import numpy as np
import ml_dtypes


def mxq(x, axis, fmt="e4m3"):
    dtype, down = {"e4m3": (ml_dtypes.float8_e4m3fn, 7), "e5m2": (ml_dtypes.float8_e5m2, 14)}[fmt]
    v = np.moveaxis(np.asarray(x, np.float32).astype(ml_dtypes.bfloat16).astype(np.float64), axis, -1)
    blocks = v.reshape(v.shape[:-1] + (-1, 32))
    amax = np.abs(blocks).max(-1, keepdims=True)
    byte = np.maximum(np.where(amax > 0, np.frexp(amax)[1] - 1 + 127, 0) - down, 1)
    scale = np.exp2(byte - 127.0)
    codes = (blocks / scale).astype(np.float32).astype(dtype).astype(np.float64)
    return np.moveaxis((codes * scale).reshape(v.shape), -1, axis)


WIDE = False


def mx_kscale(k):
    if not WIDE:
        return np.ones(k)
    levels = np.array([10, -10, 5, -5, 0])
    if k % 512:
        return np.exp2(np.random.permutation(np.resize(levels, k // 32))).repeat(32)
    a = np.empty((k // 512, 16))
    for p in range(k // 512):
        a[p, :8] = np.random.permutation(np.resize(levels, 8))
        for g in range(8):
            far = levels[np.abs(levels - a[p, g]) >= 10]
            a[p, g + 8] = far[np.random.randint(len(far))]
    return np.exp2(a.ravel()).repeat(32)


def f64(x):
    return np.asarray(x).astype(np.float64)


def striped8(idx):
    return np.concatenate([x.reshape(-1, 16).T for x in idx]).astype(np.uint16)


def runs(offs, k):
    lists = np.stack([offs[16 * r : 16 * r + 16].T.reshape(-1) for r in range(8)]).astype(np.int64)
    return lists[np.arange(k) % 512 // 64]


def pack_weight(w):
    k, n = w.shape
    w = f64(np.asarray(w, np.float32).astype(ml_dtypes.bfloat16)).reshape(k // 32, 32, n)
    amax = np.abs(w).max(1)
    byte = np.clip(np.where(amax > 0, np.frexp(amax)[1] - 1 + 127 - 7, 1), 1, 254)
    scaled = (w * np.exp2(127.0 - byte)[:, None, :]).reshape(k, n).astype(np.float32)
    words = np.ascontiguousarray(scaled.reshape(k // 512, 128, 4, n).transpose(0, 1, 3, 2)).astype(ml_dtypes.float8_e4m3fn).view(np.uint8)
    return words, np.ascontiguousarray(byte.astype(np.uint8).reshape(k // 512, 16, n))


def unpack_weight(words, scales):
    g, p, n, _ = words.shape
    vals = np.ascontiguousarray(words).view(ml_dtypes.float8_e4m3fn).astype(np.float64) * np.repeat(np.exp2(scales.astype(np.float64) - 127.0), 8, axis=1)[..., None]
    return vals.transpose(0, 1, 3, 2).reshape(g * 512, n)


def relu(v):
    return np.maximum(v, 0.0)


K, T, S, H, N = 512, 2048, 1024, 512, 256


def setup_inputs():
    n = np.random.standard_normal
    s = mx_kscale(K)[:, None]
    u = mx_kscale(H)
    packed_xT = pack_weight(n((K, T)) * s)
    return {
        "x_words": packed_xT[0],
        "x_scales": packed_xT[1],
        "w1": (n((K, H)) / np.sqrt(K) / s * u).astype(np.float32),
        "w2": (n((H, N)) / np.sqrt(H) / u[:, None]).astype(np.float32),
        "pos": (0.5 * n((H, S)) * u[:, None]).astype(np.float32),
        "offs": striped8(np.random.randint(0, T, (8, S))),
    }


def reference(x_words, x_scales, w1, w2, pos, offs):
    xq = unpack_weight(x_words, x_scales)[np.arange(K)[:, None], runs(offs, K)]
    h = relu((mxq(f64(w1), 0, "e4m3").T @ xq) + f64(pos))
    return mxq(f64(w2), 0, "e4m3").T @ mxq(h, 0, "e4m3")

@@ -1,0 +1,174 @@
+from contextlib import ExitStack
+
+import concourse.mybir as mybir
+
+K, T, S, H, N = 512, 2048, 1024, 512, 256
+FLOPS = 2 * K * H * S + 2 * H * N * S
+
+F32 = mybir.dt.float32
+BF16 = mybir.dt.bfloat16
+I32 = mybir.dt.int32
+U32 = mybir.dt.uint32
+U16 = mybir.dt.uint16
+U8 = mybir.dt.uint8
+FP8X4 = mybir.dt.float8_e4m3fn_x4
+ACT = mybir.ActivationFunctionType
+ALU = mybir.AluOpType
+
+P = 128
+PACK = 4
+CHUNK = 128
+POS_COLS = 256
+GATHER = 512
+GROUPS = ((0, 1), (2, 3), (4, 5), (6,), (7,))
+W1_VECTOR_COLS = 88
+RELU_ON_VECTOR = (0, 1, 7)
+
+
+def tile_picked_phpq_relu_p_kernel(tc, x_words, x_scales, w1, w2, pos, offs, out):
+    nc = tc.nc
+    with ExitStack() as ctx:
+        keep = ctx.enter_context(tc.tile_pool(name="keep", bufs=1))
+        ring = ctx.enter_context(tc.tile_pool(name="ring", bufs=3))
+        psum1 = ctx.enter_context(tc.psum_pool(name="psum1", bufs=4))
+        psum2 = ctx.enter_context(tc.psum_pool(name="psum2", bufs=3))
+
+        pos_rows = pos.rearrange("(p t) j -> p t j", t=PACK)
+
+        offsets = keep.tile([P, S // 16], U16, name="offsets")
+        nc.sync.dma_start(offsets[:], offs)
+
+        scale_table = keep.tile([P, T], U8, name="scale_table", tag="slot_a", align_bytes=64)
+        nc.sync.dma_start(
+            out=scale_table[:].bitcast(I32),
+            in_=x_scales[0].bitcast(I32).unsqueeze(1).to_broadcast([16, 8, T // 4]),
+        )
+
+        word_table = keep.tile([P, T], U32, name="word_table", tag="slot_b", align_bytes=64)
+        nc.sync.dma_start(out=word_table[:].bitcast(I32), in_=x_words[0].rearrange("p n t -> p (n t)").bitcast(I32))
+        w1_raw = keep.tile([P, PACK, H], F32, name="w1_raw", tag="slot_c", align_bytes=64)
+        nc.sync.dma_start(out=w1_raw[:], in_=w1.rearrange("(p j) c -> p j c", j=PACK))
+        pos_first = keep.tile([P, PACK, POS_COLS], F32, name="pos_first")
+        nc.sync.dma_start(out=pos_first[:], in_=pos_rows[:, :, 0:POS_COLS])
+
+        x_plane = keep.tile([P, S], U8, name="x_plane", align_bytes=64)
+        nc.gpsimd.memset(x_plane[:].bitcast(I32), 0)
+
+        picked_scales = keep.tile([P, S], U8, name="picked_scales", align_bytes=64)
+        nc.vector.tensor_copy(out=picked_scales[:], in_=scale_table[:].indirect(offsets[:]))
+        for r in range(PACK):
+            nc.scalar.dma_start(out=x_plane[r:P:32, :].bitcast(I32), in_=picked_scales[8 * r : P : 32, :].bitcast(I32))
+
+        late = keep.tile([P, 2, PACK * POS_COLS], F32, name="late", tag="slot_a", align_bytes=64)
+        w2_raw = late[:, 0, :].rearrange("p (j n) -> p j n", j=PACK)
+        pos_second = late[:, 1, :].rearrange("p (t j) -> p t j", t=PACK)
+        nc.sync.dma_start(out=w2_raw, in_=w2.rearrange("(p j) n -> p j n", j=PACK))
+        nc.sync.dma_start(out=pos_second, in_=pos_rows[:, :, POS_COLS : 2 * POS_COLS])
+
+        x_codes = keep.tile([P, S], U32, name="x_codes", align_bytes=64)
+        for g in range(S // GATHER):
+            nc.vector.tensor_copy(
+                out=x_codes[:, g * GATHER : (g + 1) * GATHER],
+                in_=word_table[:].indirect(offsets[:, g * GATHER // 16 : (g + 1) * GATHER // 16]),
+            )
+        pos_third = keep.tile([P, PACK, POS_COLS], F32, name="pos_third", tag="slot_b", align_bytes=64)
+        nc.sync.dma_start(out=pos_third[:], in_=pos_rows[:, :, 2 * POS_COLS : 3 * POS_COLS])
+
+        w1_bf = keep.tile([P, PACK * H], BF16, name="w1_bf", align_bytes=64)
+        w1_dst = w1_bf[:].rearrange("p (t m j) -> p m j t", t=PACK, j=PACK)
+        w1_src = w1_raw[:].rearrange("p j (m t) -> p m j t", t=PACK)
+        nc.scalar.activation(out=w1_dst[:, W1_VECTOR_COLS:P], in_=w1_src[:, W1_VECTOR_COLS:P], func=ACT.Copy)
+        nc.vector.tensor_copy(out=w1_dst[:, 0:W1_VECTOR_COLS], in_=w1_src[:, 0:W1_VECTOR_COLS])
+        pos_fourth = keep.tile([P, PACK, POS_COLS], F32, name="pos_fourth", tag="slot_c", align_bytes=64)
+        nc.sync.dma_start(out=pos_fourth[:], in_=pos_rows[:, :, 3 * POS_COLS : 4 * POS_COLS])
+        pos_tiles = (pos_first[:], pos_second, pos_third[:], pos_fourth[:])
+
+        w1_codes = keep.tile([P, H], U32, name="w1_codes", align_bytes=64)
+        w1_plane = keep.tile([P, H], U8, name="w1_plane", align_bytes=64)
+        for t in range(PACK):
+            nc.vector.quantize_mx(
+                out=w1_codes[:, t * P : (t + 1) * P].bitcast(FP8X4),
+                scales=w1_plane[:, t * P : (t + 1) * P],
+                in_=w1_bf[:, t * PACK * P : (t + 1) * PACK * P],
+            )
+
+        w2_bf = keep.tile([P, PACK * N], BF16, name="w2_bf", align_bytes=64)
+        w2_codes = keep.tile([P, N], U32, name="w2_codes", align_bytes=64)
+        w2_plane = keep.tile([P, N], U8, name="w2_plane", align_bytes=64)
+        h_sum = keep.tile([P, PACK * S], BF16, name="h_sum", align_bytes=64)
+        h_bf = keep.tile([P, PACK * S], BF16, name="h_bf", align_bytes=64)
+        h_codes = keep.tile([P, S], U32, name="h_codes", align_bytes=64)
+        h_plane = keep.tile([P, S], U8, name="h_plane", align_bytes=64)
+        out_rows = out.rearrange("(u p) j -> p u j", p=P)
+
+        def cast_w2():
+            nc.scalar.activation(
+                out=w2_bf[:].rearrange("p (c i j) -> p c j i", i=4, j=PACK),
+                in_=w2_raw.rearrange("p j (c i) -> p c j i", i=4),
+                func=ACT.Copy,
+            )
+
+        def quantize_w2():
+            nc.vector.quantize_mx(out=w2_codes[:].bitcast(FP8X4), scales=w2_plane[:], in_=w2_bf[:])
+
+        def first_layer(k):
+            cols = slice(k * CHUNK, (k + 1) * CHUNK)
+            acc = psum1.tile([P, PACK, CHUNK], F32, name="acc")
+            for t in range(PACK):
+                nc.tensor.matmul_mx(
+                    out=acc[:, t, :],
+                    lhsT=w1_codes[:, t * P : (t + 1) * P].bitcast(FP8X4),
+                    lhsT_scale=w1_plane[:, t * P : (t + 1) * P],
+                    rhs=x_codes[:, cols].bitcast(FP8X4),
+                    rhs_scale=x_plane[:, cols],
+                    start=True,
+                    stop=True,
+                )
+            first = (k * CHUNK) % POS_COLS
+            pos_part = pos_tiles[k * CHUNK // POS_COLS][:, :, first : first + CHUNK]
+            nc.vector.tensor_tensor(
+                out=h_sum[:, PACK * k * CHUNK : PACK * (k + 1) * CHUNK].rearrange("p (c i t) -> p c t i", i=4, t=PACK),
+                in0=acc[:].rearrange("p t (c i) -> p c t i", i=4),
+                in1=pos_part.rearrange("p t (c i) -> p c t i", i=4),
+                op=ALU.add,
+            )
+
+        def relu(k):
+            wide = slice(PACK * k * CHUNK, PACK * (k + 1) * CHUNK)
+            if k in RELU_ON_VECTOR:
+                nc.vector.tensor_scalar_max(out=h_bf[:, wide], in0=h_sum[:, wide], scalar1=0.0)
+            else:
+                nc.scalar.activation(out=h_bf[:, wide], in_=h_sum[:, wide], func=ACT.Relu)
+
+        def second_layer(group):
+            lo, hi = group[0] * CHUNK, (group[-1] + 1) * CHUNK
+            nc.vector.quantize_mx(
+                out=h_codes[:, lo:hi].bitcast(FP8X4), scales=h_plane[:, lo:hi], in_=h_bf[:, PACK * lo : PACK * hi]
+            )
+            res = psum2.tile([P, N // P, hi - lo], F32, name="res")
+            for u in range(N // P):
+                nc.tensor.matmul_mx(
+                    out=res[:, u, :],
+                    lhsT=w2_codes[:, u * P : (u + 1) * P].bitcast(FP8X4),
+                    lhsT_scale=w2_plane[:, u * P : (u + 1) * P],
+                    rhs=h_codes[:, lo:hi].bitcast(FP8X4),
+                    rhs_scale=h_plane[:, lo:hi],
+                    start=True,
+                    stop=True,
+                )
+            staged = ring.tile([P, N // P, hi - lo], F32, name="staged")
+            nc.scalar.copy(out=staged[:], in_=res[:])
+            nc.sync.dma_start(out=out_rows[:, :, lo:hi], in_=staged[:])
+
+        chunks = S // CHUNK
+        cast_w2()
+        for k in range(chunks + 2):
+            if k < chunks:
+                first_layer(k)
+            if 1 <= k <= chunks:
+                relu(k - 1)
+            if k == 2:
+                quantize_w2()
+            for group in GROUPS:
+                if group[-1] == k - 2:
+                    second_layer(group)

@@ -19,9 +19,8 @@ P = 128
 PACK = 4
 CHUNK = 128
 POS_COLS = 256
-GATHER = 512
+EARLY = 768
 GROUPS = ((0, 1), (2, 3), (4, 5), (6,), (7,))
-W1_VECTOR_COLS = 88
 RELU_ON_VECTOR = (0, 1, 7)
 
 
@@ -29,16 +28,16 @@ def tile_picked_phpq_relu_p_kernel(tc, x_words, x_scales, w1, w2, pos, offs, out
     nc = tc.nc
     with ExitStack() as ctx:
         keep = ctx.enter_context(tc.tile_pool(name="keep", bufs=1))
-        ring = ctx.enter_context(tc.tile_pool(name="ring", bufs=3))
+        reuse = ctx.enter_context(tc.tile_pool(name="reuse", bufs=1))
         psum1 = ctx.enter_context(tc.psum_pool(name="psum1", bufs=4))
-        psum2 = ctx.enter_context(tc.psum_pool(name="psum2", bufs=3))
+        psum2 = ctx.enter_context(tc.psum_pool(name="psum2", bufs=4))
 
         pos_rows = pos.rearrange("(p t) j -> p t j", t=PACK)
 
         offsets = keep.tile([P, S // 16], U16, name="offsets")
         nc.sync.dma_start(offsets[:], offs)
 
-        scale_table = keep.tile([P, T], U8, name="scale_table", tag="slot_a", align_bytes=64)
+        scale_table = reuse.tile([P, T], U8, name="scale_table", offset=3072)
         nc.sync.dma_start(
             out=scale_table[:].bitcast(I32),
             in_=x_scales[0].bitcast(I32).unsqueeze(1).to_broadcast([16, 8, T // 4]),
@@ -48,40 +47,42 @@ def tile_picked_phpq_relu_p_kernel(tc, x_words, x_scales, w1, w2, pos, offs, out
         nc.sync.dma_start(out=word_table[:].bitcast(I32), in_=x_words[0].rearrange("p n t -> p (n t)").bitcast(I32))
         w1_raw = keep.tile([P, PACK, H], F32, name="w1_raw", tag="slot_c", align_bytes=64)
         nc.sync.dma_start(out=w1_raw[:], in_=w1.rearrange("(p j) c -> p j c", j=PACK))
-        pos_first = keep.tile([P, PACK, POS_COLS], F32, name="pos_first")
-        nc.sync.dma_start(out=pos_first[:], in_=pos_rows[:, :, 0:POS_COLS])
+
+        def load_pos(c, pool, **place):
+            tile = pool.tile([P, PACK, POS_COLS], F32, name=f"pos{c}", **place)
+            nc.sync.dma_start(out=tile[:], in_=pos_rows[:, :, c * POS_COLS : (c + 1) * POS_COLS])
+            return tile
+
+        pos_tiles = []
+        pos_tiles.append(load_pos(0, keep))
 
         x_plane = keep.tile([P, S], U8, name="x_plane", align_bytes=64)
         nc.gpsimd.memset(x_plane[:].bitcast(I32), 0)
 
-        picked_scales = keep.tile([P, S], U8, name="picked_scales", align_bytes=64)
+        picked_scales = keep.tile([P, S], U8, name="picked_scales", tag="slot_e", align_bytes=64)
         nc.vector.tensor_copy(out=picked_scales[:], in_=scale_table[:].indirect(offsets[:]))
         for r in range(PACK):
-            nc.scalar.dma_start(out=x_plane[r:P:32, :].bitcast(I32), in_=picked_scales[8 * r : P : 32, :].bitcast(I32))
+            nc.sync.dma_start(out=x_plane[r:P:32, :].bitcast(I32), in_=picked_scales[8 * r : P : 32, :].bitcast(I32))
 
-        late = keep.tile([P, 2, PACK * POS_COLS], F32, name="late", tag="slot_a", align_bytes=64)
-        w2_raw = late[:, 0, :].rearrange("p (j n) -> p j n", j=PACK)
-        pos_second = late[:, 1, :].rearrange("p (t j) -> p t j", t=PACK)
-        nc.sync.dma_start(out=w2_raw, in_=w2.rearrange("(p j) n -> p j n", j=PACK))
-        nc.sync.dma_start(out=pos_second, in_=pos_rows[:, :, POS_COLS : 2 * POS_COLS])
+        w2_raw = reuse.tile([P, PACK, N], F32, name="w2_raw", offset=4096)
+        nc.sync.dma_start(out=w2_raw[:], in_=w2.rearrange("(p j) n -> p j n", j=PACK))
+        pos_tiles.append(load_pos(1, reuse, offset=0))
 
-        x_codes = keep.tile([P, S], U32, name="x_codes", align_bytes=64)
-        for g in range(S // GATHER):
-            nc.vector.tensor_copy(
-                out=x_codes[:, g * GATHER : (g + 1) * GATHER],
-                in_=word_table[:].indirect(offsets[:, g * GATHER // 16 : (g + 1) * GATHER // 16]),
-            )
-        pos_third = keep.tile([P, PACK, POS_COLS], F32, name="pos_third", tag="slot_b", align_bytes=64)
-        nc.sync.dma_start(out=pos_third[:], in_=pos_rows[:, :, 2 * POS_COLS : 3 * POS_COLS])
+        def gather_words(dst, lo, hi):
+            nc.vector.tensor_copy(out=dst, in_=word_table[:].indirect(offsets[:, lo // 16 : hi // 16]))
 
-        w1_bf = keep.tile([P, PACK * H], BF16, name="w1_bf", align_bytes=64)
-        w1_dst = w1_bf[:].rearrange("p (t m j) -> p m j t", t=PACK, j=PACK)
+        x_early = keep.tile([P, EARLY], U32, name="x_early", align_bytes=64)
+        gather_words(x_early[:], 0, EARLY)
+
         w1_src = w1_raw[:].rearrange("p j (m t) -> p m j t", t=PACK)
-        nc.scalar.activation(out=w1_dst[:, W1_VECTOR_COLS:P], in_=w1_src[:, W1_VECTOR_COLS:P], func=ACT.Copy)
-        nc.vector.tensor_copy(out=w1_dst[:, 0:W1_VECTOR_COLS], in_=w1_src[:, 0:W1_VECTOR_COLS])
-        pos_fourth = keep.tile([P, PACK, POS_COLS], F32, name="pos_fourth", tag="slot_c", align_bytes=64)
-        nc.sync.dma_start(out=pos_fourth[:], in_=pos_rows[:, :, 3 * POS_COLS : 4 * POS_COLS])
-        pos_tiles = (pos_first[:], pos_second, pos_third[:], pos_fourth[:])
+        w1_lo = keep.tile([P, 2 * H], BF16, name="w1_lo", align_bytes=64)
+        w1_hi = keep.tile([P, 2 * H], BF16, name="w1_hi", tag="slot_d", align_bytes=64)
+        nc.vector.tensor_copy(out=w1_lo[:].rearrange("p (t m j) -> p m j t", t=2, j=PACK), in_=w1_src[:, :, :, 0:2])
+        nc.scalar.activation(
+            out=w1_hi[:].rearrange("p (t m j) -> p m j t", t=2, j=PACK), in_=w1_src[:, :, :, 2:PACK], func=ACT.Copy
+        )
+        pos_tiles.append(load_pos(2, keep, tag="slot_e", align_bytes=64))
+        pos_tiles.append(load_pos(3, keep, tag="slot_c", align_bytes=64))
 
         w1_codes = keep.tile([P, H], U32, name="w1_codes", align_bytes=64)
         w1_plane = keep.tile([P, H], U8, name="w1_plane", align_bytes=64)
@@ -89,22 +90,28 @@ def tile_picked_phpq_relu_p_kernel(tc, x_words, x_scales, w1, w2, pos, offs, out
             nc.vector.quantize_mx(
                 out=w1_codes[:, t * P : (t + 1) * P].bitcast(FP8X4),
                 scales=w1_plane[:, t * P : (t + 1) * P],
-                in_=w1_bf[:, t * PACK * P : (t + 1) * PACK * P],
+                in_=(w1_lo, w1_hi)[t // 2][:, (t % 2) * H : (t % 2 + 1) * H],
             )
+
+        x_late = keep.tile([P, S - EARLY], U32, name="x_late", tag="slot_d", align_bytes=64)
+        gather_words(x_late[:], EARLY, S)
 
         w2_bf = keep.tile([P, PACK * N], BF16, name="w2_bf", align_bytes=64)
         w2_codes = keep.tile([P, N], U32, name="w2_codes", align_bytes=64)
         w2_plane = keep.tile([P, N], U8, name="w2_plane", align_bytes=64)
-        h_sum = keep.tile([P, PACK * S], BF16, name="h_sum", align_bytes=64)
-        h_bf = keep.tile([P, PACK * S], BF16, name="h_bf", align_bytes=64)
-        h_codes = keep.tile([P, S], U32, name="h_codes", align_bytes=64)
-        h_plane = keep.tile([P, S], U8, name="h_plane", align_bytes=64)
         out_rows = out.rearrange("(u p) j -> p u j", p=P)
+        h_sum, h_bf = {}, {}
+        for group in GROUPS:
+            whole = keep.tile([P, PACK * CHUNK * len(group)], BF16, name=f"h_bf{group[0]}", align_bytes=64)
+            h_bf[group] = whole
+            for n, k in enumerate(group):
+                h_bf[k] = whole[:, n * PACK * CHUNK : (n + 1) * PACK * CHUNK]
+                h_sum[k] = keep.tile([P, PACK * CHUNK], BF16, name=f"h_sum{k}", align_bytes=64)
 
         def cast_w2():
             nc.scalar.activation(
                 out=w2_bf[:].rearrange("p (c i j) -> p c j i", i=4, j=PACK),
-                in_=w2_raw.rearrange("p j (c i) -> p c j i", i=4),
+                in_=w2_raw[:].rearrange("p j (c i) -> p c j i", i=4),
                 func=ACT.Copy,
             )
 
@@ -113,13 +120,14 @@ def tile_picked_phpq_relu_p_kernel(tc, x_words, x_scales, w1, w2, pos, offs, out
 
         def first_layer(k):
             cols = slice(k * CHUNK, (k + 1) * CHUNK)
+            x_part = x_early[:, cols] if k * CHUNK < EARLY else x_late[:, k * CHUNK - EARLY : (k + 1) * CHUNK - EARLY]
             acc = psum1.tile([P, PACK, CHUNK], F32, name="acc")
             for t in range(PACK):
                 nc.tensor.matmul_mx(
                     out=acc[:, t, :],
                     lhsT=w1_codes[:, t * P : (t + 1) * P].bitcast(FP8X4),
                     lhsT_scale=w1_plane[:, t * P : (t + 1) * P],
-                    rhs=x_codes[:, cols].bitcast(FP8X4),
+                    rhs=x_part.bitcast(FP8X4),
                     rhs_scale=x_plane[:, cols],
                     start=True,
                     stop=True,
@@ -127,37 +135,42 @@ def tile_picked_phpq_relu_p_kernel(tc, x_words, x_scales, w1, w2, pos, offs, out
             first = (k * CHUNK) % POS_COLS
             pos_part = pos_tiles[k * CHUNK // POS_COLS][:, :, first : first + CHUNK]
             nc.vector.tensor_tensor(
-                out=h_sum[:, PACK * k * CHUNK : PACK * (k + 1) * CHUNK].rearrange("p (c i t) -> p c t i", i=4, t=PACK),
+                out=h_sum[k][:].rearrange("p (c i t) -> p c t i", i=4, t=PACK),
                 in0=acc[:].rearrange("p t (c i) -> p c t i", i=4),
                 in1=pos_part.rearrange("p t (c i) -> p c t i", i=4),
                 op=ALU.add,
             )
 
         def relu(k):
-            wide = slice(PACK * k * CHUNK, PACK * (k + 1) * CHUNK)
             if k in RELU_ON_VECTOR:
-                nc.vector.tensor_scalar_max(out=h_bf[:, wide], in0=h_sum[:, wide], scalar1=0.0)
+                nc.vector.tensor_scalar_max(out=h_bf[k], in0=h_sum[k][:], scalar1=0.0)
             else:
-                nc.scalar.activation(out=h_bf[:, wide], in_=h_sum[:, wide], func=ACT.Relu)
+                nc.scalar.activation(out=h_bf[k], in_=h_sum[k][:], func=ACT.Relu)
 
         def second_layer(group):
             lo, hi = group[0] * CHUNK, (group[-1] + 1) * CHUNK
-            nc.vector.quantize_mx(
-                out=h_codes[:, lo:hi].bitcast(FP8X4), scales=h_plane[:, lo:hi], in_=h_bf[:, PACK * lo : PACK * hi]
-            )
+            h_codes = keep.tile([P, hi - lo], U32, name=f"h_codes{lo}", align_bytes=64)
+            h_plane = keep.tile([P, hi - lo], U8, name=f"h_plane{lo}", align_bytes=64)
+            nc.vector.quantize_mx(out=h_codes[:].bitcast(FP8X4), scales=h_plane[:], in_=h_bf[group][:])
+            staged = keep.tile([P, N // P, hi - lo], F32, name=f"staged{lo}")
+            last = group == GROUPS[-1]
             res = psum2.tile([P, N // P, hi - lo], F32, name="res")
+            banks = (res, psum2.tile([P, N // P, hi - lo], F32, name="res")) if last else (res, res)
             for u in range(N // P):
                 nc.tensor.matmul_mx(
-                    out=res[:, u, :],
+                    out=banks[u][:, u, :],
                     lhsT=w2_codes[:, u * P : (u + 1) * P].bitcast(FP8X4),
                     lhsT_scale=w2_plane[:, u * P : (u + 1) * P],
-                    rhs=h_codes[:, lo:hi].bitcast(FP8X4),
-                    rhs_scale=h_plane[:, lo:hi],
+                    rhs=h_codes[:].bitcast(FP8X4),
+                    rhs_scale=h_plane[:],
                     start=True,
                     stop=True,
                 )
-            staged = ring.tile([P, N // P, hi - lo], F32, name="staged")
-            nc.scalar.copy(out=staged[:], in_=res[:])
+            if last:
+                nc.scalar.copy(out=staged[:, 0, :], in_=banks[0][:, 0, :])
+                nc.vector.tensor_copy(out=staged[:, 1, :], in_=banks[1][:, 1, :])
+            else:
+                nc.scalar.copy(out=staged[:], in_=res[:])
             nc.sync.dma_start(out=out_rows[:, :, lo:hi], in_=staged[:])
 
         chunks = S // CHUNK

@@ -20,8 +20,8 @@ PACK = 4
 CHUNK = 128
 POS_COLS = 256
 EARLY = 768
-GROUPS = ((0, 1), (2, 3), (4, 5), (6,), (7,))
-RELU_ON_VECTOR = (0, 1, 7)
+GROUPS = ((0, 1), (2, 3), (4,), (5,), (6,), (7,))
+RELU_ON_VECTOR = (0, 5, 6, 7)
 
 
 def tile_picked_phpq_relu_p_kernel(tc, x_words, x_scales, w1, w2, pos, offs, out):
@@ -169,19 +169,33 @@ def tile_picked_phpq_relu_p_kernel(tc, x_words, x_scales, w1, w2, pos, offs, out
             if last:
                 nc.scalar.copy(out=staged[:, 0, :], in_=banks[0][:, 0, :])
                 nc.vector.tensor_copy(out=staged[:, 1, :], in_=banks[1][:, 1, :])
+            elif group == GROUPS[-2]:
+                nc.vector.tensor_copy(out=staged[:], in_=res[:])
             else:
                 nc.scalar.copy(out=staged[:], in_=res[:])
             nc.sync.dma_start(out=out_rows[:, :, lo:hi], in_=staged[:])
 
-        chunks = S // CHUNK
         cast_w2()
-        for k in range(chunks + 2):
-            if k < chunks:
-                first_layer(k)
-            if 1 <= k <= chunks:
-                relu(k - 1)
-            if k == 2:
-                quantize_w2()
-            for group in GROUPS:
-                if group[-1] == k - 2:
-                    second_layer(group)
+        first_layer(0)
+        first_layer(1)
+        relu(0)
+        first_layer(2)
+        relu(1)
+        quantize_w2()
+        first_layer(3)
+        relu(2)
+        second_layer(GROUPS[0])
+        first_layer(4)
+        relu(3)
+        first_layer(5)
+        relu(4)
+        second_layer(GROUPS[1])
+        first_layer(6)
+        relu(5)
+        second_layer(GROUPS[2])
+        second_layer(GROUPS[3])
+        first_layer(7)
+        relu(6)
+        relu(7)
+        second_layer(GROUPS[4])
+        second_layer(GROUPS[5])

@@ -21,7 +21,7 @@ CHUNK = 128
 POS_COLS = 256
 EARLY = 768
 GROUPS = ((0, 1), (2, 3), (4,), (5,), (6,), (7,))
-RELU_ON_VECTOR = (0, 5, 6, 7)
+RELU_ON_VECTOR = (5, 6, 7)
 
 
 def tile_picked_phpq_relu_p_kernel(tc, x_words, x_scales, w1, w2, pos, offs, out):
@@ -54,7 +54,8 @@ def tile_picked_phpq_relu_p_kernel(tc, x_words, x_scales, w1, w2, pos, offs, out
             return tile
 
         pos_tiles = []
-        pos_tiles.append(load_pos(0, keep))
+        w2_raw = keep.tile([P, PACK, N], F32, name="w2_raw")
+        nc.sync.dma_start(out=w2_raw[:], in_=w2.rearrange("(p j) n -> p j n", j=PACK))
 
         x_plane = keep.tile([P, S], U8, name="x_plane", align_bytes=64)
         nc.gpsimd.memset(x_plane[:].bitcast(I32), 0)
@@ -64,8 +65,7 @@ def tile_picked_phpq_relu_p_kernel(tc, x_words, x_scales, w1, w2, pos, offs, out
         for r in range(PACK):
             nc.sync.dma_start(out=x_plane[r:P:32, :].bitcast(I32), in_=picked_scales[8 * r : P : 32, :].bitcast(I32))
 
-        w2_raw = reuse.tile([P, PACK, N], F32, name="w2_raw", offset=4096)
-        nc.sync.dma_start(out=w2_raw[:], in_=w2.rearrange("(p j) n -> p j n", j=PACK))
+        pos_tiles.append(load_pos(0, reuse, offset=4096))
         pos_tiles.append(load_pos(1, reuse, offset=0))
 
         def gather_words(dst, lo, hi):
@@ -176,12 +176,12 @@ def tile_picked_phpq_relu_p_kernel(tc, x_words, x_scales, w1, w2, pos, offs, out
             nc.sync.dma_start(out=out_rows[:, :, lo:hi], in_=staged[:])
 
         cast_w2()
+        quantize_w2()
         first_layer(0)
         first_layer(1)
         relu(0)
         first_layer(2)
         relu(1)
-        quantize_w2()
         first_layer(3)
         relu(2)
         second_layer(GROUPS[0])

@@ -135,9 +135,9 @@ def tile_picked_phpq_relu_p_kernel(tc, x_words, x_scales, w1, w2, pos, offs, out
             first = (k * CHUNK) % POS_COLS
             pos_part = pos_tiles[k * CHUNK // POS_COLS][:, :, first : first + CHUNK]
             nc.vector.tensor_tensor(
-                out=h_sum[k][:].rearrange("p (c i t) -> p c t i", i=4, t=PACK),
-                in0=acc[:].rearrange("p t (c i) -> p c t i", i=4),
-                in1=pos_part.rearrange("p t (c i) -> p c t i", i=4),
+                out=h_sum[k][:].rearrange("p (c i t) -> p c t i", i=2, t=PACK),
+                in0=acc[:].rearrange("p t (c i) -> p c t i", i=2),
+                in1=pos_part.rearrange("p t (c i) -> p c t i", i=2),
                 op=ALU.add,
             )
 

@@ -17,11 +17,12 @@ ALU = mybir.AluOpType
 
 P = 128
 PACK = 4
-CHUNK = 128
-POS_COLS = 256
 EARLY = 768
+CHUNKS = tuple((128 * k, 128 * k + 128) for k in range(8))
+POS_PIECES = ((0, 256), (256, 512), (512, 768), (768, 1024))
 GROUPS = ((0, 1), (2, 3), (4,), (5,), (6,), (7,))
-RELU_ON_VECTOR = (5, 6, 7)
+RELU_ON_VECTOR = (6, 7)
+WALK = 2
 
 
 def tile_picked_phpq_relu_p_kernel(tc, x_words, x_scales, w1, w2, pos, offs, out):
@@ -47,13 +48,6 @@ def tile_picked_phpq_relu_p_kernel(tc, x_words, x_scales, w1, w2, pos, offs, out
         nc.sync.dma_start(out=word_table[:].bitcast(I32), in_=x_words[0].rearrange("p n t -> p (n t)").bitcast(I32))
         w1_raw = keep.tile([P, PACK, H], F32, name="w1_raw", tag="slot_c", align_bytes=64)
         nc.sync.dma_start(out=w1_raw[:], in_=w1.rearrange("(p j) c -> p j c", j=PACK))
-
-        def load_pos(c, pool, **place):
-            tile = pool.tile([P, PACK, POS_COLS], F32, name=f"pos{c}", **place)
-            nc.sync.dma_start(out=tile[:], in_=pos_rows[:, :, c * POS_COLS : (c + 1) * POS_COLS])
-            return tile
-
-        pos_tiles = []
         w2_raw = keep.tile([P, PACK, N], F32, name="w2_raw")
         nc.sync.dma_start(out=w2_raw[:], in_=w2.rearrange("(p j) n -> p j n", j=PACK))
 
@@ -65,8 +59,13 @@ def tile_picked_phpq_relu_p_kernel(tc, x_words, x_scales, w1, w2, pos, offs, out
         for r in range(PACK):
             nc.sync.dma_start(out=x_plane[r:P:32, :].bitcast(I32), in_=picked_scales[8 * r : P : 32, :].bitcast(I32))
 
-        pos_tiles.append(load_pos(0, reuse, offset=4096))
-        pos_tiles.append(load_pos(1, reuse, offset=0))
+        pos_all = reuse.tile([P, PACK * S], F32, name="pos_all", offset=4096)
+
+        def pos_piece(lo, hi):
+            return pos_all[:, PACK * lo : PACK * hi].rearrange("p (t j) -> p t j", t=PACK)
+
+        for lo, hi in POS_PIECES:
+            nc.sync.dma_start(out=pos_piece(lo, hi), in_=pos_rows[:, :, lo:hi])
 
         def gather_words(dst, lo, hi):
             nc.vector.tensor_copy(out=dst, in_=word_table[:].indirect(offsets[:, lo // 16 : hi // 16]))
@@ -81,16 +80,15 @@ def tile_picked_phpq_relu_p_kernel(tc, x_words, x_scales, w1, w2, pos, offs, out
         nc.scalar.activation(
             out=w1_hi[:].rearrange("p (t m j) -> p m j t", t=2, j=PACK), in_=w1_src[:, :, :, 2:PACK], func=ACT.Copy
         )
-        pos_tiles.append(load_pos(2, keep, tag="slot_e", align_bytes=64))
-        pos_tiles.append(load_pos(3, keep, tag="slot_c", align_bytes=64))
+
 
         w1_codes = keep.tile([P, H], U32, name="w1_codes", align_bytes=64)
         w1_plane = keep.tile([P, H], U8, name="w1_plane", align_bytes=64)
-        for t in range(PACK):
+        for half, source in enumerate((w1_lo, w1_hi)):
             nc.vector.quantize_mx(
-                out=w1_codes[:, t * P : (t + 1) * P].bitcast(FP8X4),
-                scales=w1_plane[:, t * P : (t + 1) * P],
-                in_=(w1_lo, w1_hi)[t // 2][:, (t % 2) * H : (t % 2 + 1) * H],
+                out=w1_codes[:, half * 2 * P : (half + 1) * 2 * P].bitcast(FP8X4),
+                scales=w1_plane[:, half * 2 * P : (half + 1) * 2 * P],
+                in_=source[:],
             )
 
         x_late = keep.tile([P, S - EARLY], U32, name="x_late", tag="slot_d", align_bytes=64)
@@ -102,42 +100,48 @@ def tile_picked_phpq_relu_p_kernel(tc, x_words, x_scales, w1, w2, pos, offs, out
         out_rows = out.rearrange("(u p) j -> p u j", p=P)
         h_sum, h_bf = {}, {}
         for group in GROUPS:
-            whole = keep.tile([P, PACK * CHUNK * len(group)], BF16, name=f"h_bf{group[0]}", align_bytes=64)
+            base = CHUNKS[group[0]][0]
+            whole = keep.tile([P, PACK * (CHUNKS[group[-1]][1] - base)], BF16, name=f"h_bf{group[0]}", align_bytes=64)
             h_bf[group] = whole
-            for n, k in enumerate(group):
-                h_bf[k] = whole[:, n * PACK * CHUNK : (n + 1) * PACK * CHUNK]
-                h_sum[k] = keep.tile([P, PACK * CHUNK], BF16, name=f"h_sum{k}", align_bytes=64)
+            for k in group:
+                lo, hi = CHUNKS[k]
+                h_bf[k] = whole[:, PACK * (lo - base) : PACK * (hi - base)]
+                h_sum[k] = keep.tile([P, PACK * (hi - lo)], BF16, name=f"h_sum{k}", align_bytes=64)
 
-        def cast_w2():
+        def cast_w2(u):
             nc.scalar.activation(
-                out=w2_bf[:].rearrange("p (c i j) -> p c j i", i=4, j=PACK),
-                in_=w2_raw[:].rearrange("p j (c i) -> p c j i", i=4),
+                out=w2_bf[:, u * PACK * P : (u + 1) * PACK * P].rearrange("p (c i j) -> p c j i", i=4, j=PACK),
+                in_=w2_raw[:, :, u * P : (u + 1) * P].rearrange("p j (c i) -> p c j i", i=4),
                 func=ACT.Copy,
             )
 
-        def quantize_w2():
-            nc.vector.quantize_mx(out=w2_codes[:].bitcast(FP8X4), scales=w2_plane[:], in_=w2_bf[:])
+        def quantize_w2(u):
+            nc.vector.quantize_mx(
+                out=w2_codes[:, u * P : (u + 1) * P].bitcast(FP8X4),
+                scales=w2_plane[:, u * P : (u + 1) * P],
+                in_=w2_bf[:, u * PACK * P : (u + 1) * PACK * P],
+            )
 
         def first_layer(k):
-            cols = slice(k * CHUNK, (k + 1) * CHUNK)
-            x_part = x_early[:, cols] if k * CHUNK < EARLY else x_late[:, k * CHUNK - EARLY : (k + 1) * CHUNK - EARLY]
-            acc = psum1.tile([P, PACK, CHUNK], F32, name="acc")
+            lo, hi = CHUNKS[k]
+            x_part = x_early[:, lo:hi] if lo < EARLY else x_late[:, lo - EARLY : hi - EARLY]
+            acc = psum1.tile([P, PACK, hi - lo], F32, name="acc")
             for t in range(PACK):
                 nc.tensor.matmul_mx(
                     out=acc[:, t, :],
                     lhsT=w1_codes[:, t * P : (t + 1) * P].bitcast(FP8X4),
                     lhsT_scale=w1_plane[:, t * P : (t + 1) * P],
                     rhs=x_part.bitcast(FP8X4),
-                    rhs_scale=x_plane[:, cols],
+                    rhs_scale=x_plane[:, lo:hi],
                     start=True,
                     stop=True,
                 )
-            first = (k * CHUNK) % POS_COLS
-            pos_part = pos_tiles[k * CHUNK // POS_COLS][:, :, first : first + CHUNK]
+            first, end = max(piece for piece in POS_PIECES if piece[0] <= lo)
+            pos_part = pos_piece(first, end)[:, :, lo - first : hi - first]
             nc.vector.tensor_tensor(
-                out=h_sum[k][:].rearrange("p (c i t) -> p c t i", i=2, t=PACK),
-                in0=acc[:].rearrange("p t (c i) -> p c t i", i=2),
-                in1=pos_part.rearrange("p t (c i) -> p c t i", i=2),
+                out=h_sum[k][:].rearrange("p (c i t) -> p c t i", i=WALK, t=PACK),
+                in0=acc[:].rearrange("p t (c i) -> p c t i", i=WALK),
+                in1=pos_part.rearrange("p t (c i) -> p c t i", i=WALK),
                 op=ALU.add,
             )
 
@@ -147,13 +151,15 @@ def tile_picked_phpq_relu_p_kernel(tc, x_words, x_scales, w1, w2, pos, offs, out
             else:
                 nc.scalar.activation(out=h_bf[k], in_=h_sum[k][:], func=ACT.Relu)
 
-        def second_layer(group):
-            lo, hi = group[0] * CHUNK, (group[-1] + 1) * CHUNK
+        products = {}
+
+        def second_layer(g):
+            group = GROUPS[g]
+            lo, hi = CHUNKS[group[0]][0], CHUNKS[group[-1]][1]
             h_codes = keep.tile([P, hi - lo], U32, name=f"h_codes{lo}", align_bytes=64)
             h_plane = keep.tile([P, hi - lo], U8, name=f"h_plane{lo}", align_bytes=64)
             nc.vector.quantize_mx(out=h_codes[:].bitcast(FP8X4), scales=h_plane[:], in_=h_bf[group][:])
-            staged = keep.tile([P, N // P, hi - lo], F32, name=f"staged{lo}")
-            last = group == GROUPS[-1]
+            last = g == len(GROUPS) - 1
             res = psum2.tile([P, N // P, hi - lo], F32, name="res")
             banks = (res, psum2.tile([P, N // P, hi - lo], F32, name="res")) if last else (res, res)
             for u in range(N // P):
@@ -166,36 +172,51 @@ def tile_picked_phpq_relu_p_kernel(tc, x_words, x_scales, w1, w2, pos, offs, out
                     start=True,
                     stop=True,
                 )
-            if last:
+            products[g] = banks
+
+        def store(g, on_vector=False):
+            group = GROUPS[g]
+            lo, hi = CHUNKS[group[0]][0], CHUNKS[group[-1]][1]
+            banks = products[g]
+            staged = keep.tile([P, N // P, hi - lo], F32, name=f"staged{lo}")
+            if g == len(GROUPS) - 1:
                 nc.scalar.copy(out=staged[:, 0, :], in_=banks[0][:, 0, :])
                 nc.vector.tensor_copy(out=staged[:, 1, :], in_=banks[1][:, 1, :])
-            elif group == GROUPS[-2]:
-                nc.vector.tensor_copy(out=staged[:], in_=res[:])
+            elif on_vector:
+                nc.vector.tensor_copy(out=staged[:], in_=banks[0][:])
             else:
-                nc.scalar.copy(out=staged[:], in_=res[:])
+                nc.scalar.copy(out=staged[:], in_=banks[0][:])
             nc.sync.dma_start(out=out_rows[:, :, lo:hi], in_=staged[:])
 
-        cast_w2()
-        quantize_w2()
+        cast_w2(0)
+        cast_w2(1)
+        quantize_w2(0)
         first_layer(0)
+        quantize_w2(1)
         first_layer(1)
         relu(0)
         first_layer(2)
         relu(1)
         first_layer(3)
         relu(2)
-        second_layer(GROUPS[0])
+        second_layer(0)
         first_layer(4)
         relu(3)
+        store(0)
         first_layer(5)
         relu(4)
-        second_layer(GROUPS[1])
-        first_layer(6)
+        second_layer(1)
         relu(5)
-        second_layer(GROUPS[2])
-        second_layer(GROUPS[3])
+        first_layer(6)
+        store(1)
+        second_layer(2)
         first_layer(7)
+        second_layer(3)
+        store(2)
         relu(6)
         relu(7)
-        second_layer(GROUPS[4])
-        second_layer(GROUPS[5])
+        store(3)
+        second_layer(4)
+        second_layer(5)
+        store(4, True)
+        store(5)

@@ -39,15 +39,18 @@ def tile_picked_phpq_relu_p_kernel(tc, x_words, x_scales, w1, w2, pos, offs, out
         nc.sync.dma_start(offsets[:], offs)
 
         scale_table = reuse.tile([P, T], U8, name="scale_table", offset=3072)
-        nc.sync.dma_start(
-            out=scale_table[:].bitcast(I32),
-            in_=x_scales[0].bitcast(I32).unsqueeze(1).to_broadcast([16, 8, T // 4]),
-        )
+        nc.vector.memset(scale_table[:, 0:1152].bitcast(I32), 0)
+        nc.gpsimd.memset(scale_table[:, 1152:T].bitcast(I32), 0)
+        w1_rows = w1.rearrange("(p j) c -> p j c", j=PACK)
+        w1_raw = keep.tile([P, PACK, H], F32, name="w1_raw", align_bytes=64)
+        nc.sync.dma_start(out=w1_raw[:, 0:1, :], in_=w1_rows[:, 0:1, :])
+        warm = keep.tile([P, 1], BF16, name="warm")
+        nc.scalar.activation(out=warm[:], in_=w1_raw[:, 0, 0:1], func=ACT.Copy)
+        nc.sync.dma_start(out=scale_table[0:P:8, :].bitcast(I32), in_=x_scales[0].bitcast(I32))
 
         word_table = keep.tile([P, T], U32, name="word_table", tag="slot_b", align_bytes=64)
         nc.sync.dma_start(out=word_table[:].bitcast(I32), in_=x_words[0].rearrange("p n t -> p (n t)").bitcast(I32))
-        w1_raw = keep.tile([P, PACK, H], F32, name="w1_raw", tag="slot_c", align_bytes=64)
-        nc.sync.dma_start(out=w1_raw[:], in_=w1.rearrange("(p j) c -> p j c", j=PACK))
+        nc.sync.dma_start(out=w1_raw[:, 1:PACK, :], in_=w1_rows[:, 1:PACK, :])
         w2_raw = keep.tile([P, PACK, N], F32, name="w2_raw")
         nc.sync.dma_start(out=w2_raw[:], in_=w2.rearrange("(p j) n -> p j n", j=PACK))
 

@@ -39,8 +39,7 @@ def tile_picked_phpq_relu_p_kernel(tc, x_words, x_scales, w1, w2, pos, offs, out
         nc.sync.dma_start(offsets[:], offs)
 
         scale_table = reuse.tile([P, T], U8, name="scale_table", offset=3072)
-        nc.vector.memset(scale_table[:, 0:1152].bitcast(I32), 0)
-        nc.gpsimd.memset(scale_table[:, 1152:T].bitcast(I32), 0)
+        nc.vector.memset(scale_table[:].bitcast(I32), 0)
         w1_rows = w1.rearrange("(p j) c -> p j c", j=PACK)
         w1_raw = keep.tile([P, PACK, H], F32, name="w1_raw", align_bytes=64)
         nc.sync.dma_start(out=w1_raw[:, 0:1, :], in_=w1_rows[:, 0:1, :])
@@ -55,7 +54,7 @@ def tile_picked_phpq_relu_p_kernel(tc, x_words, x_scales, w1, w2, pos, offs, out
         nc.sync.dma_start(out=w2_raw[:], in_=w2.rearrange("(p j) n -> p j n", j=PACK))
 
         x_plane = keep.tile([P, S], U8, name="x_plane", align_bytes=64)
-        nc.gpsimd.memset(x_plane[:].bitcast(I32), 0)
+        nc.vector.memset(x_plane[:].bitcast(I32), 0)
 
         picked_scales = keep.tile([P, S], U8, name="picked_scales", tag="slot_e", align_bytes=64)
         nc.vector.tensor_copy(out=picked_scales[:], in_=scale_table[:].indirect(offsets[:]))

@@ -19,7 +19,7 @@ P = 128
 PACK = 4
 EARLY = 768
 CHUNKS = tuple((128 * k, 128 * k + 128) for k in range(8))
-POS_PIECES = ((0, 256), (256, 512), (512, 768), (768, 1024))
+POS_PIECES = ((0, 256), (256, 512), (512, 768), (768, 896), (896, 1024))
 GROUPS = ((0, 1), (2, 3), (4,), (5,), (6,), (7,))
 RELU_ON_VECTOR = (6, 7)
 WALK = 2
@@ -161,9 +161,9 @@ def tile_picked_phpq_relu_p_kernel(tc, x_words, x_scales, w1, w2, pos, offs, out
             h_codes = keep.tile([P, hi - lo], U32, name=f"h_codes{lo}", align_bytes=64)
             h_plane = keep.tile([P, hi - lo], U8, name=f"h_plane{lo}", align_bytes=64)
             nc.vector.quantize_mx(out=h_codes[:].bitcast(FP8X4), scales=h_plane[:], in_=h_bf[group][:])
-            last = g == len(GROUPS) - 1
+            last = g >= len(GROUPS) - 2
             res = psum2.tile([P, N // P, hi - lo], F32, name="res")
-            banks = (res, psum2.tile([P, N // P, hi - lo], F32, name="res")) if last else (res, res)
+            banks = (res, psum1.tile([P, N // P, hi - lo], F32, name="acc")) if last else (res, res)
             for u in range(N // P):
                 nc.tensor.matmul_mx(
                     out=banks[u][:, u, :],
@@ -181,9 +181,15 @@ def tile_picked_phpq_relu_p_kernel(tc, x_words, x_scales, w1, w2, pos, offs, out
             lo, hi = CHUNKS[group[0]][0], CHUNKS[group[-1]][1]
             banks = products[g]
             staged = keep.tile([P, N // P, hi - lo], F32, name=f"staged{lo}")
-            if g == len(GROUPS) - 1:
+            if g == len(GROUPS) - 2:
                 nc.scalar.copy(out=staged[:, 0, :], in_=banks[0][:, 0, :])
                 nc.vector.tensor_copy(out=staged[:, 1, :], in_=banks[1][:, 1, :])
+            elif g == len(GROUPS) - 1:
+                nc.scalar.copy(out=staged[:, 0, :], in_=banks[0][:, 0, :])
+                nc.vector.tensor_copy(out=staged[:, 1, :], in_=banks[1][:, 1, :])
+                nc.scalar.dma_start(out=out_rows[:, 0, lo:hi], in_=staged[:, 0, :])
+                nc.sync.dma_start(out=out_rows[:, 1, lo:hi], in_=staged[:, 1, :])
+                return
             elif on_vector:
                 nc.vector.tensor_copy(out=staged[:], in_=banks[0][:])
             else:

@@ -181,15 +181,9 @@ def tile_picked_phpq_relu_p_kernel(tc, x_words, x_scales, w1, w2, pos, offs, out
             lo, hi = CHUNKS[group[0]][0], CHUNKS[group[-1]][1]
             banks = products[g]
             staged = keep.tile([P, N // P, hi - lo], F32, name=f"staged{lo}")
-            if g == len(GROUPS) - 2:
+            if g >= len(GROUPS) - 2:
                 nc.scalar.copy(out=staged[:, 0, :], in_=banks[0][:, 0, :])
                 nc.vector.tensor_copy(out=staged[:, 1, :], in_=banks[1][:, 1, :])
-            elif g == len(GROUPS) - 1:
-                nc.scalar.copy(out=staged[:, 0, :], in_=banks[0][:, 0, :])
-                nc.vector.tensor_copy(out=staged[:, 1, :], in_=banks[1][:, 1, :])
-                nc.scalar.dma_start(out=out_rows[:, 0, lo:hi], in_=staged[:, 0, :])
-                nc.sync.dma_start(out=out_rows[:, 1, lo:hi], in_=staged[:, 1, :])
-                return
             elif on_vector:
                 nc.vector.tensor_copy(out=staged[:], in_=banks[0][:])
             else:

@@ -19,7 +19,7 @@ P = 128
 PACK = 4
 EARLY = 768
 CHUNKS = tuple((128 * k, 128 * k + 128) for k in range(8))
-POS_PIECES = ((0, 256), (256, 512), (512, 768), (768, 896), (896, 1024))
+POS_PIECES = ((0, 256), (256, 512), (512, 768), (768, 1024))
 GROUPS = ((0, 1), (2, 3), (4,), (5,), (6,), (7,))
 RELU_ON_VECTOR = (6, 7)
 WALK = 2
@@ -43,8 +43,6 @@ def tile_picked_phpq_relu_p_kernel(tc, x_words, x_scales, w1, w2, pos, offs, out
         w1_rows = w1.rearrange("(p j) c -> p j c", j=PACK)
         w1_raw = keep.tile([P, PACK, H], F32, name="w1_raw", align_bytes=64)
         nc.sync.dma_start(out=w1_raw[:, 0:1, :], in_=w1_rows[:, 0:1, :])
-        warm = keep.tile([P, 1], BF16, name="warm")
-        nc.scalar.activation(out=warm[:], in_=w1_raw[:, 0, 0:1], func=ACT.Copy)
         nc.sync.dma_start(out=scale_table[0:P:8, :].bitcast(I32), in_=x_scales[0].bitcast(I32))
 
         word_table = keep.tile([P, T], U32, name="word_table", tag="slot_b", align_bytes=64)
@@ -79,9 +77,9 @@ def tile_picked_phpq_relu_p_kernel(tc, x_words, x_scales, w1, w2, pos, offs, out
         w1_lo = keep.tile([P, 2 * H], BF16, name="w1_lo", align_bytes=64)
         w1_hi = keep.tile([P, 2 * H], BF16, name="w1_hi", tag="slot_d", align_bytes=64)
         nc.vector.tensor_copy(out=w1_lo[:].rearrange("p (t m j) -> p m j t", t=2, j=PACK), in_=w1_src[:, :, :, 0:2])
-        nc.scalar.activation(
-            out=w1_hi[:].rearrange("p (t m j) -> p m j t", t=2, j=PACK), in_=w1_src[:, :, :, 2:PACK], func=ACT.Copy
-        )
+        w1_hi_dst = w1_hi[:].rearrange("p (t m j) -> p m j t", t=2, j=PACK)
+        nc.scalar.activation(out=w1_hi_dst[:, :, 0, :], in_=w1_src[:, :, 0, 2:PACK], func=ACT.Copy)
+        nc.scalar.activation(out=w1_hi_dst[:, :, 1:PACK, :], in_=w1_src[:, :, 1:PACK, 2:PACK], func=ACT.Copy)
 
 
         w1_codes = keep.tile([P, H], U32, name="w1_codes", align_bytes=64)

@@ -17,12 +17,13 @@ ALU = mybir.AluOpType
 
 P = 128
 PACK = 4
-EARLY = 768
+EARLY = 512
 CHUNKS = tuple((128 * k, 128 * k + 128) for k in range(8))
 POS_PIECES = ((0, 256), (256, 512), (512, 768), (768, 1024))
 GROUPS = ((0, 1), (2, 3), (4,), (5,), (6,), (7,))
 RELU_ON_VECTOR = (6, 7)
 WALK = 2
+SLIVER = 8
 
 
 def tile_picked_phpq_relu_p_kernel(tc, x_words, x_scales, w1, w2, pos, offs, out):
@@ -30,6 +31,7 @@ def tile_picked_phpq_relu_p_kernel(tc, x_words, x_scales, w1, w2, pos, offs, out
     with ExitStack() as ctx:
         keep = ctx.enter_context(tc.tile_pool(name="keep", bufs=1))
         reuse = ctx.enter_context(tc.tile_pool(name="reuse", bufs=1))
+        raw = ctx.enter_context(tc.tile_pool(name="raw", bufs=1))
         psum1 = ctx.enter_context(tc.psum_pool(name="psum1", bufs=4))
         psum2 = ctx.enter_context(tc.psum_pool(name="psum2", bufs=4))
 
@@ -41,13 +43,12 @@ def tile_picked_phpq_relu_p_kernel(tc, x_words, x_scales, w1, w2, pos, offs, out
         scale_table = reuse.tile([P, T], U8, name="scale_table", offset=3072)
         nc.vector.memset(scale_table[:].bitcast(I32), 0)
         w1_rows = w1.rearrange("(p j) c -> p j c", j=PACK)
-        w1_raw = keep.tile([P, PACK, H], F32, name="w1_raw", align_bytes=64)
+        w1_raw = raw.tile([P, PACK, H], F32, name="w1_raw", align_bytes=64, offset=0)
         nc.sync.dma_start(out=w1_raw[:, 0:1, :], in_=w1_rows[:, 0:1, :])
         nc.sync.dma_start(out=scale_table[0:P:8, :].bitcast(I32), in_=x_scales[0].bitcast(I32))
-
-        word_table = keep.tile([P, T], U32, name="word_table", tag="slot_b", align_bytes=64)
-        nc.sync.dma_start(out=word_table[:].bitcast(I32), in_=x_words[0].rearrange("p n t -> p (n t)").bitcast(I32))
         nc.sync.dma_start(out=w1_raw[:, 1:PACK, :], in_=w1_rows[:, 1:PACK, :])
+        word_table = keep.tile([P, T], U32, name="word_table", align_bytes=64)
+        nc.sync.dma_start(out=word_table[:].bitcast(I32), in_=x_words[0].rearrange("p n t -> p (n t)").bitcast(I32))
         w2_raw = keep.tile([P, PACK, N], F32, name="w2_raw")
         nc.sync.dma_start(out=w2_raw[:], in_=w2.rearrange("(p j) n -> p j n", j=PACK))
 
@@ -70,28 +71,30 @@ def tile_picked_phpq_relu_p_kernel(tc, x_words, x_scales, w1, w2, pos, offs, out
         def gather_words(dst, lo, hi):
             nc.vector.tensor_copy(out=dst, in_=word_table[:].indirect(offsets[:, lo // 16 : hi // 16]))
 
-        x_early = keep.tile([P, EARLY], U32, name="x_early", align_bytes=64)
-        gather_words(x_early[:], 0, EARLY)
-
         w1_src = w1_raw[:].rearrange("p j (m t) -> p m j t", t=PACK)
         w1_lo = keep.tile([P, 2 * H], BF16, name="w1_lo", align_bytes=64)
-        w1_hi = keep.tile([P, 2 * H], BF16, name="w1_hi", tag="slot_d", align_bytes=64)
+        w1_hi = keep.tile([P, 2 * H], BF16, name="w1_hi", align_bytes=64)
         nc.vector.tensor_copy(out=w1_lo[:].rearrange("p (t m j) -> p m j t", t=2, j=PACK), in_=w1_src[:, :, :, 0:2])
         w1_hi_dst = w1_hi[:].rearrange("p (t m j) -> p m j t", t=2, j=PACK)
-        nc.scalar.activation(out=w1_hi_dst[:, :, 0, :], in_=w1_src[:, :, 0, 2:PACK], func=ACT.Copy)
-        nc.scalar.activation(out=w1_hi_dst[:, :, 1:PACK, :], in_=w1_src[:, :, 1:PACK, 2:PACK], func=ACT.Copy)
+        for columns, rows in ((slice(0, SLIVER), slice(0, 1)), (slice(SLIVER, P), slice(0, PACK)), (slice(0, SLIVER), slice(1, PACK))):
+            nc.scalar.activation(out=w1_hi_dst[:, columns, rows, :], in_=w1_src[:, columns, rows, 2:PACK], func=ACT.Copy)
 
 
         w1_codes = keep.tile([P, H], U32, name="w1_codes", align_bytes=64)
-        w1_plane = keep.tile([P, H], U8, name="w1_plane", align_bytes=64)
-        for half, source in enumerate((w1_lo, w1_hi)):
+        w1_planes = (
+            raw.tile([P, 2 * P], U8, name="w1_plane_lo", align_bytes=64, offset=4 * S),
+            keep.tile([P, 2 * P], U8, name="w1_plane_hi", align_bytes=64),
+        )
+        for half, source in ((1, w1_hi), (0, w1_lo)):
             nc.vector.quantize_mx(
                 out=w1_codes[:, half * 2 * P : (half + 1) * 2 * P].bitcast(FP8X4),
-                scales=w1_plane[:, half * 2 * P : (half + 1) * 2 * P],
+                scales=w1_planes[half][:],
                 in_=source[:],
             )
 
-        x_late = keep.tile([P, S - EARLY], U32, name="x_late", tag="slot_d", align_bytes=64)
+        x_early = raw.tile([P, EARLY], U32, name="x_early", align_bytes=64, offset=0)
+        gather_words(x_early[:], 0, EARLY)
+        x_late = raw.tile([P, S - EARLY], U32, name="x_late", align_bytes=64, offset=4 * EARLY)
         gather_words(x_late[:], EARLY, S)
 
         w2_bf = keep.tile([P, PACK * N], BF16, name="w2_bf", align_bytes=64)
@@ -130,7 +133,7 @@ def tile_picked_phpq_relu_p_kernel(tc, x_words, x_scales, w1, w2, pos, offs, out
                 nc.tensor.matmul_mx(
                     out=acc[:, t, :],
                     lhsT=w1_codes[:, t * P : (t + 1) * P].bitcast(FP8X4),
-                    lhsT_scale=w1_plane[:, t * P : (t + 1) * P],
+                    lhsT_scale=w1_planes[t // 2][:, t % 2 * P : (t % 2 + 1) * P],
                     rhs=x_part.bitcast(FP8X4),
                     rhs_scale=x_plane[:, lo:hi],
                     start=True,

@@ -19,7 +19,7 @@ P = 128
 PACK = 4
 EARLY = 512
 CHUNKS = tuple((128 * k, 128 * k + 128) for k in range(8))
-POS_PIECES = ((0, 256), (256, 512), (512, 768), (768, 1024))
+POS_PIECES = ((0, 256), (256, 512), (512, 768), (768, 896), (896, 1024))
 GROUPS = ((0, 1), (2, 3), (4,), (5,), (6,), (7,))
 RELU_ON_VECTOR = (6, 7)
 WALK = 2
@@ -213,13 +213,13 @@ def tile_picked_phpq_relu_p_kernel(tc, x_words, x_scales, w1, w2, pos, offs, out
         first_layer(6)
         store(1)
         second_layer(2)
+        relu(6)
         first_layer(7)
         second_layer(3)
         store(2)
-        relu(6)
+        second_layer(4)
         relu(7)
         store(3)
-        second_layer(4)
         second_layer(5)
         store(4, True)
         store(5)

@@ -20,8 +20,9 @@ PACK = 4
 EARLY = 512
 CHUNKS = tuple((128 * k, 128 * k + 128) for k in range(8))
 POS_PIECES = ((0, 256), (256, 512), (512, 768), (768, 896), (896, 1024))
-GROUPS = ((0, 1), (2, 3), (4,), (5,), (6,), (7,))
+GROUPS = ((0,), (1,), (2, 3), (4,), (5,), (6,), (7,))
 RELU_ON_VECTOR = (6, 7)
+FIRST_SHARED_GROUP = 4
 WALK = 2
 SLIVER = 8
 
@@ -162,7 +163,7 @@ def tile_picked_phpq_relu_p_kernel(tc, x_words, x_scales, w1, w2, pos, offs, out
             h_codes = keep.tile([P, hi - lo], U32, name=f"h_codes{lo}", align_bytes=64)
             h_plane = keep.tile([P, hi - lo], U8, name=f"h_plane{lo}", align_bytes=64)
             nc.vector.quantize_mx(out=h_codes[:].bitcast(FP8X4), scales=h_plane[:], in_=h_bf[group][:])
-            last = g >= len(GROUPS) - 2
+            last = g >= FIRST_SHARED_GROUP
             res = psum2.tile([P, N // P, hi - lo], F32, name="res")
             banks = (res, psum1.tile([P, N // P, hi - lo], F32, name="acc")) if last else (res, res)
             for u in range(N // P):
@@ -182,7 +183,7 @@ def tile_picked_phpq_relu_p_kernel(tc, x_words, x_scales, w1, w2, pos, offs, out
             lo, hi = CHUNKS[group[0]][0], CHUNKS[group[-1]][1]
             banks = products[g]
             staged = keep.tile([P, N // P, hi - lo], F32, name=f"staged{lo}")
-            if g >= len(GROUPS) - 2:
+            if g >= FIRST_SHARED_GROUP:
                 nc.scalar.copy(out=staged[:, 0, :], in_=banks[0][:, 0, :])
                 nc.vector.tensor_copy(out=staged[:, 1, :], in_=banks[1][:, 1, :])
             elif on_vector:
@@ -200,26 +201,28 @@ def tile_picked_phpq_relu_p_kernel(tc, x_words, x_scales, w1, w2, pos, offs, out
         relu(0)
         first_layer(2)
         relu(1)
+        second_layer(0)
         first_layer(3)
         relu(2)
-        second_layer(0)
+        store(0)
+        second_layer(1)
         first_layer(4)
         relu(3)
-        store(0)
+        store(1)
         first_layer(5)
         relu(4)
-        second_layer(1)
+        second_layer(2)
         relu(5)
         first_layer(6)
-        store(1)
-        second_layer(2)
-        relu(6)
-        first_layer(7)
-        second_layer(3)
         store(2)
+        second_layer(3)
+        first_layer(7)
+        relu(6)
         second_layer(4)
         relu(7)
         store(3)
         second_layer(5)
-        store(4, True)
+        second_layer(6)
+        store(4)
         store(5)
+        store(6)

@@ -17,7 +17,7 @@ ALU = mybir.AluOpType
 
 P = 128
 PACK = 4
-EARLY = 512
+EARLY = 384
 CHUNKS = tuple((128 * k, 128 * k + 128) for k in range(8))
 POS_PIECES = ((0, 256), (256, 512), (512, 768), (768, 896), (896, 1024))
 GROUPS = ((0,), (1,), (2, 3), (4,), (5,), (6,), (7,))
@@ -98,14 +98,17 @@ def tile_picked_phpq_relu_p_kernel(tc, x_words, x_scales, w1, w2, pos, offs, out
         x_late = raw.tile([P, S - EARLY], U32, name="x_late", align_bytes=64, offset=4 * EARLY)
         gather_words(x_late[:], EARLY, S)
 
-        w2_bf = keep.tile([P, PACK * N], BF16, name="w2_bf", align_bytes=64)
-        w2_codes = keep.tile([P, N], U32, name="w2_codes", align_bytes=64)
-        w2_plane = keep.tile([P, N], U8, name="w2_plane", align_bytes=64)
+        w2_bf = keep.tile([P, PACK * (N + P)], BF16, name="w2_bf", align_bytes=64)
+        w2_codes = keep.tile([P, N + P], U32, name="w2_codes", align_bytes=64)
+        w2_plane = keep.tile([P, N + P], U8, name="w2_plane", align_bytes=64)
         out_rows = out.rearrange("(u p) j -> p u j", p=P)
         h_sum, h_bf = {}, {}
         for group in GROUPS:
             base = CHUNKS[group[0]][0]
-            whole = keep.tile([P, PACK * (CHUNKS[group[-1]][1] - base)], BF16, name=f"h_bf{group[0]}", align_bytes=64)
+            if group == (0,):
+                whole = w2_bf[:, PACK * N : PACK * (N + P)]
+            else:
+                whole = keep.tile([P, PACK * (CHUNKS[group[-1]][1] - base)], BF16, name=f"h_bf{group[0]}", align_bytes=64)
             h_bf[group] = whole
             for k in group:
                 lo, hi = CHUNKS[k]
@@ -160,9 +163,15 @@ def tile_picked_phpq_relu_p_kernel(tc, x_words, x_scales, w1, w2, pos, offs, out
         def second_layer(g):
             group = GROUPS[g]
             lo, hi = CHUNKS[group[0]][0], CHUNKS[group[-1]][1]
-            h_codes = keep.tile([P, hi - lo], U32, name=f"h_codes{lo}", align_bytes=64)
-            h_plane = keep.tile([P, hi - lo], U8, name=f"h_plane{lo}", align_bytes=64)
-            nc.vector.quantize_mx(out=h_codes[:].bitcast(FP8X4), scales=h_plane[:], in_=h_bf[group][:])
+            if g == 0:
+                h_codes, h_plane = w2_codes[:, N : N + P], w2_plane[:, N : N + P]
+                nc.vector.quantize_mx(
+                    out=w2_codes[:, P : N + P].bitcast(FP8X4), scales=w2_plane[:, P : N + P], in_=w2_bf[:, PACK * P : PACK * (N + P)]
+                )
+            else:
+                h_codes = keep.tile([P, hi - lo], U32, name=f"h_codes{lo}", align_bytes=64)
+                h_plane = keep.tile([P, hi - lo], U8, name=f"h_plane{lo}", align_bytes=64)
+                nc.vector.quantize_mx(out=h_codes[:].bitcast(FP8X4), scales=h_plane[:], in_=h_bf[group][:])
             last = g >= FIRST_SHARED_GROUP
             res = psum2.tile([P, N // P, hi - lo], F32, name="res")
             banks = (res, psum1.tile([P, N // P, hi - lo], F32, name="acc")) if last else (res, res)
@@ -196,7 +205,6 @@ def tile_picked_phpq_relu_p_kernel(tc, x_words, x_scales, w1, w2, pos, offs, out
         cast_w2(1)
         quantize_w2(0)
         first_layer(0)
-        quantize_w2(1)
         first_layer(1)
         relu(0)
         first_layer(2)

@@ -33,8 +33,8 @@ def tile_picked_phpq_relu_p_kernel(tc, x_words, x_scales, w1, w2, pos, offs, out
         keep = ctx.enter_context(tc.tile_pool(name="keep", bufs=1))
         reuse = ctx.enter_context(tc.tile_pool(name="reuse", bufs=1))
         raw = ctx.enter_context(tc.tile_pool(name="raw", bufs=1))
-        psum1 = ctx.enter_context(tc.psum_pool(name="psum1", bufs=4))
-        psum2 = ctx.enter_context(tc.psum_pool(name="psum2", bufs=4))
+        psum1 = ctx.enter_context(tc.psum_pool(name="psum1", bufs=3))
+        psum2 = ctx.enter_context(tc.psum_pool(name="psum2", bufs=5))
 
         pos_rows = pos.rearrange("(p t) j -> p t j", t=PACK)
 

@@ -25,6 +25,8 @@ RELU_ON_VECTOR = (6, 7)
 FIRST_SHARED_GROUP = 4
 WALK = 2
 SLIVER = 8
+FRONT = 256
+SHARE = 32
 
 
 def tile_picked_phpq_relu_p_kernel(tc, x_words, x_scales, w1, w2, pos, offs, out):
@@ -45,9 +47,10 @@ def tile_picked_phpq_relu_p_kernel(tc, x_words, x_scales, w1, w2, pos, offs, out
         nc.vector.memset(scale_table[:].bitcast(I32), 0)
         w1_rows = w1.rearrange("(p j) c -> p j c", j=PACK)
         w1_raw = raw.tile([P, PACK, H], F32, name="w1_raw", align_bytes=64, offset=0)
-        nc.sync.dma_start(out=w1_raw[:, 0:1, :], in_=w1_rows[:, 0:1, :])
+        w1_flat, w1_hbm = w1_raw[:].rearrange("p j c -> p (j c)"), w1_rows.rearrange("p j c -> p (j c)")
+        nc.sync.dma_start(out=w1_flat[:, 0:FRONT], in_=w1_hbm[:, 0:FRONT])
         nc.sync.dma_start(out=scale_table[0:P:8, :].bitcast(I32), in_=x_scales[0].bitcast(I32))
-        nc.sync.dma_start(out=w1_raw[:, 1:PACK, :], in_=w1_rows[:, 1:PACK, :])
+        nc.sync.dma_start(out=w1_flat[:, FRONT:], in_=w1_hbm[:, FRONT:])
         word_table = keep.tile([P, T], U32, name="word_table", align_bytes=64)
         nc.sync.dma_start(out=word_table[:].bitcast(I32), in_=x_words[0].rearrange("p n t -> p (n t)").bitcast(I32))
         w2_raw = keep.tile([P, PACK, N], F32, name="w2_raw")
@@ -75,9 +78,11 @@ def tile_picked_phpq_relu_p_kernel(tc, x_words, x_scales, w1, w2, pos, offs, out
         w1_src = w1_raw[:].rearrange("p j (m t) -> p m j t", t=PACK)
         w1_lo = keep.tile([P, 2 * H], BF16, name="w1_lo", align_bytes=64)
         w1_hi = keep.tile([P, 2 * H], BF16, name="w1_hi", align_bytes=64)
-        nc.vector.tensor_copy(out=w1_lo[:].rearrange("p (t m j) -> p m j t", t=2, j=PACK), in_=w1_src[:, :, :, 0:2])
         w1_hi_dst = w1_hi[:].rearrange("p (t m j) -> p m j t", t=2, j=PACK)
-        for columns, rows in ((slice(0, SLIVER), slice(0, 1)), (slice(SLIVER, P), slice(0, PACK)), (slice(0, SLIVER), slice(1, PACK))):
+        nc.vector.tensor_copy(out=w1_hi_dst[:, 0:SHARE, :, :], in_=w1_src[:, 0:SHARE, :, 2:PACK])
+        nc.vector.tensor_copy(out=w1_lo[:].rearrange("p (t m j) -> p m j t", t=2, j=PACK), in_=w1_src[:, :, :, 0:2])
+        sliver = slice(SHARE, SHARE + SLIVER)
+        for columns, rows in ((sliver, slice(0, 1)), (slice(SHARE + SLIVER, P), slice(0, PACK)), (sliver, slice(1, PACK))):
             nc.scalar.activation(out=w1_hi_dst[:, columns, rows, :], in_=w1_src[:, columns, rows, 2:PACK], func=ACT.Copy)
 
 

@@ -26,7 +26,7 @@ FIRST_SHARED_GROUP = 4
 WALK = 2
 SLIVER = 8
 FRONT = 256
-SHARE = 32
+SHARE = 16
 
 
 def tile_picked_phpq_relu_p_kernel(tc, x_words, x_scales, w1, w2, pos, offs, out):
@@ -57,11 +57,11 @@ def tile_picked_phpq_relu_p_kernel(tc, x_words, x_scales, w1, w2, pos, offs, out
         nc.sync.dma_start(out=w2_raw[:], in_=w2.rearrange("(p j) n -> p j n", j=PACK))
 
         x_plane = keep.tile([P, S], U8, name="x_plane", align_bytes=64)
-        nc.vector.memset(x_plane[:].bitcast(I32), 0)
 
         picked_scales = keep.tile([P, S], U8, name="picked_scales", tag="slot_e", align_bytes=64)
         nc.vector.tensor_copy(out=picked_scales[:], in_=scale_table[:].indirect(offsets[:]))
-        for r in range(PACK):
+        nc.vector.tensor_copy(out=x_plane[:].bitcast(I32), in_=picked_scales[:].bitcast(I32))
+        for r in range(1, PACK):
             nc.sync.dma_start(out=x_plane[r:P:32, :].bitcast(I32), in_=picked_scales[8 * r : P : 32, :].bitcast(I32))
 
         pos_all = reuse.tile([P, PACK * S], F32, name="pos_all", offset=4096)

@@ -41,7 +41,6 @@ def tile_picked_phpq_relu_p_kernel(tc, x_words, x_scales, w1, w2, pos, offs, out
         pos_rows = pos.rearrange("(p t) j -> p t j", t=PACK)
 
         offsets = keep.tile([P, S // 16], U16, name="offsets")
-        nc.sync.dma_start(offsets[:], offs)
 
         scale_table = reuse.tile([P, T], U8, name="scale_table", offset=3072)
         nc.vector.memset(scale_table[:].bitcast(I32), 0)
@@ -49,6 +48,7 @@ def tile_picked_phpq_relu_p_kernel(tc, x_words, x_scales, w1, w2, pos, offs, out
         w1_raw = raw.tile([P, PACK, H], F32, name="w1_raw", align_bytes=64, offset=0)
         w1_flat, w1_hbm = w1_raw[:].rearrange("p j c -> p (j c)"), w1_rows.rearrange("p j c -> p (j c)")
         nc.sync.dma_start(out=w1_flat[:, 0:FRONT], in_=w1_hbm[:, 0:FRONT])
+        nc.sync.dma_start(offsets[:], offs)
         nc.sync.dma_start(out=scale_table[0:P:8, :].bitcast(I32), in_=x_scales[0].bitcast(I32))
         nc.sync.dma_start(out=w1_flat[:, FRONT:], in_=w1_hbm[:, FRONT:])
         word_table = keep.tile([P, T], U32, name="word_table", align_bytes=64)

from contextlib import ExitStack

import concourse.mybir as mybir

K, T, S, H, N = 512, 2048, 1024, 512, 256
FLOPS = 2 * K * H * S + 2 * H * N * S

F32 = mybir.dt.float32
BF16 = mybir.dt.bfloat16
I32 = mybir.dt.int32
U32 = mybir.dt.uint32
U16 = mybir.dt.uint16
U8 = mybir.dt.uint8
FP8X4 = mybir.dt.float8_e4m3fn_x4
ACT = mybir.ActivationFunctionType
ALU = mybir.AluOpType

P = 128
PACK = 4
EARLY = 384
CHUNKS = tuple((128 * k, 128 * k + 128) for k in range(8))
POS_PIECES = ((0, 256), (256, 512), (512, 768), (768, 896), (896, 1024))
GROUPS = ((0,), (1,), (2, 3), (4,), (5,), (6,), (7,))
RELU_ON_VECTOR = (6, 7)
FIRST_SHARED_GROUP = 4
WALK = 2
SLIVER = 8
FRONT = 256
SHARE = 16


def tile_picked_phpq_relu_p_kernel(tc, x_words, x_scales, w1, w2, pos, offs, out):
    nc = tc.nc
    with ExitStack() as ctx:
        keep = ctx.enter_context(tc.tile_pool(name="keep", bufs=1))
        reuse = ctx.enter_context(tc.tile_pool(name="reuse", bufs=1))
        raw = ctx.enter_context(tc.tile_pool(name="raw", bufs=1))
        psum1 = ctx.enter_context(tc.psum_pool(name="psum1", bufs=3))
        psum2 = ctx.enter_context(tc.psum_pool(name="psum2", bufs=5))

        pos_rows = pos.rearrange("(p t) j -> p t j", t=PACK)

        offsets = keep.tile([P, S // 16], U16, name="offsets")

        scale_table = reuse.tile([P, T], U8, name="scale_table", offset=3072)
        nc.vector.memset(scale_table[:].bitcast(I32), 0)
        w1_rows = w1.rearrange("(p j) c -> p j c", j=PACK)
        w1_raw = raw.tile([P, PACK, H], F32, name="w1_raw", align_bytes=64, offset=0)
        w1_flat, w1_hbm = w1_raw[:].rearrange("p j c -> p (j c)"), w1_rows.rearrange("p j c -> p (j c)")
        nc.sync.dma_start(out=w1_flat[:, 0:FRONT], in_=w1_hbm[:, 0:FRONT])
        nc.sync.dma_start(offsets[:], offs)
        nc.sync.dma_start(out=scale_table[0:P:8, :].bitcast(I32), in_=x_scales[0].bitcast(I32))
        nc.sync.dma_start(out=w1_flat[:, FRONT:], in_=w1_hbm[:, FRONT:])
        word_table = keep.tile([P, T], U32, name="word_table", align_bytes=64)
        nc.sync.dma_start(out=word_table[:].bitcast(I32), in_=x_words[0].rearrange("p n t -> p (n t)").bitcast(I32))
        w2_raw = keep.tile([P, PACK, N], F32, name="w2_raw")
        nc.sync.dma_start(out=w2_raw[:], in_=w2.rearrange("(p j) n -> p j n", j=PACK))

        x_plane = keep.tile([P, S], U8, name="x_plane", align_bytes=64)

        picked_scales = keep.tile([P, S], U8, name="picked_scales", tag="slot_e", align_bytes=64)
        nc.vector.tensor_copy(out=picked_scales[:], in_=scale_table[:].indirect(offsets[:]))
        nc.vector.tensor_copy(out=x_plane[:].bitcast(I32), in_=picked_scales[:].bitcast(I32))
        for r in range(1, PACK):
            nc.sync.dma_start(out=x_plane[r:P:32, :].bitcast(I32), in_=picked_scales[8 * r : P : 32, :].bitcast(I32))

        pos_all = reuse.tile([P, PACK * S], F32, name="pos_all", offset=4096)

        def pos_piece(lo, hi):
            return pos_all[:, PACK * lo : PACK * hi].rearrange("p (t j) -> p t j", t=PACK)

        for lo, hi in POS_PIECES:
            nc.sync.dma_start(out=pos_piece(lo, hi), in_=pos_rows[:, :, lo:hi])

        def gather_words(dst, lo, hi):
            nc.vector.tensor_copy(out=dst, in_=word_table[:].indirect(offsets[:, lo // 16 : hi // 16]))

        w1_src = w1_raw[:].rearrange("p j (m t) -> p m j t", t=PACK)
        w1_lo = keep.tile([P, 2 * H], BF16, name="w1_lo", align_bytes=64)
        w1_hi = keep.tile([P, 2 * H], BF16, name="w1_hi", align_bytes=64)
        w1_hi_dst = w1_hi[:].rearrange("p (t m j) -> p m j t", t=2, j=PACK)
        nc.vector.tensor_copy(out=w1_hi_dst[:, 0:SHARE, :, :], in_=w1_src[:, 0:SHARE, :, 2:PACK])
        nc.vector.tensor_copy(out=w1_lo[:].rearrange("p (t m j) -> p m j t", t=2, j=PACK), in_=w1_src[:, :, :, 0:2])
        sliver = slice(SHARE, SHARE + SLIVER)
        for columns, rows in ((sliver, slice(0, 1)), (slice(SHARE + SLIVER, P), slice(0, PACK)), (sliver, slice(1, PACK))):
            nc.scalar.activation(out=w1_hi_dst[:, columns, rows, :], in_=w1_src[:, columns, rows, 2:PACK], func=ACT.Copy)


        w1_codes = keep.tile([P, H], U32, name="w1_codes", align_bytes=64)
        w1_planes = (
            raw.tile([P, 2 * P], U8, name="w1_plane_lo", align_bytes=64, offset=4 * S),
            keep.tile([P, 2 * P], U8, name="w1_plane_hi", align_bytes=64),
        )
        for half, source in ((1, w1_hi), (0, w1_lo)):
            nc.vector.quantize_mx(
                out=w1_codes[:, half * 2 * P : (half + 1) * 2 * P].bitcast(FP8X4),
                scales=w1_planes[half][:],
                in_=source[:],
            )

        x_early = raw.tile([P, EARLY], U32, name="x_early", align_bytes=64, offset=0)
        gather_words(x_early[:], 0, EARLY)
        x_late = raw.tile([P, S - EARLY], U32, name="x_late", align_bytes=64, offset=4 * EARLY)
        gather_words(x_late[:], EARLY, S)

        w2_bf = keep.tile([P, PACK * (N + P)], BF16, name="w2_bf", align_bytes=64)
        w2_codes = keep.tile([P, N + P], U32, name="w2_codes", align_bytes=64)
        w2_plane = keep.tile([P, N + P], U8, name="w2_plane", align_bytes=64)
        out_rows = out.rearrange("(u p) j -> p u j", p=P)
        h_sum, h_bf = {}, {}
        for group in GROUPS:
            base = CHUNKS[group[0]][0]
            if group == (0,):
                whole = w2_bf[:, PACK * N : PACK * (N + P)]
            else:
                whole = keep.tile([P, PACK * (CHUNKS[group[-1]][1] - base)], BF16, name=f"h_bf{group[0]}", align_bytes=64)
            h_bf[group] = whole
            for k in group:
                lo, hi = CHUNKS[k]
                h_bf[k] = whole[:, PACK * (lo - base) : PACK * (hi - base)]
                h_sum[k] = keep.tile([P, PACK * (hi - lo)], BF16, name=f"h_sum{k}", align_bytes=64)

        def cast_w2(u):
            nc.scalar.activation(
                out=w2_bf[:, u * PACK * P : (u + 1) * PACK * P].rearrange("p (c i j) -> p c j i", i=4, j=PACK),
                in_=w2_raw[:, :, u * P : (u + 1) * P].rearrange("p j (c i) -> p c j i", i=4),
                func=ACT.Copy,
            )

        def quantize_w2(u):
            nc.vector.quantize_mx(
                out=w2_codes[:, u * P : (u + 1) * P].bitcast(FP8X4),
                scales=w2_plane[:, u * P : (u + 1) * P],
                in_=w2_bf[:, u * PACK * P : (u + 1) * PACK * P],
            )

        def first_layer(k):
            lo, hi = CHUNKS[k]
            x_part = x_early[:, lo:hi] if lo < EARLY else x_late[:, lo - EARLY : hi - EARLY]
            acc = psum1.tile([P, PACK, hi - lo], F32, name="acc")
            for t in range(PACK):
                nc.tensor.matmul_mx(
                    out=acc[:, t, :],
                    lhsT=w1_codes[:, t * P : (t + 1) * P].bitcast(FP8X4),
                    lhsT_scale=w1_planes[t // 2][:, t % 2 * P : (t % 2 + 1) * P],
                    rhs=x_part.bitcast(FP8X4),
                    rhs_scale=x_plane[:, lo:hi],
                    start=True,
                    stop=True,
                )
            first, end = max(piece for piece in POS_PIECES if piece[0] <= lo)
            pos_part = pos_piece(first, end)[:, :, lo - first : hi - first]
            nc.vector.tensor_tensor(
                out=h_sum[k][:].rearrange("p (c i t) -> p c t i", i=WALK, t=PACK),
                in0=acc[:].rearrange("p t (c i) -> p c t i", i=WALK),
                in1=pos_part.rearrange("p t (c i) -> p c t i", i=WALK),
                op=ALU.add,
            )

        def relu(k):
            if k in RELU_ON_VECTOR:
                nc.vector.tensor_scalar_max(out=h_bf[k], in0=h_sum[k][:], scalar1=0.0)
            else:
                nc.scalar.activation(out=h_bf[k], in_=h_sum[k][:], func=ACT.Relu)

        products = {}

        def second_layer(g):
            group = GROUPS[g]
            lo, hi = CHUNKS[group[0]][0], CHUNKS[group[-1]][1]
            if g == 0:
                h_codes, h_plane = w2_codes[:, N : N + P], w2_plane[:, N : N + P]
                nc.vector.quantize_mx(
                    out=w2_codes[:, P : N + P].bitcast(FP8X4), scales=w2_plane[:, P : N + P], in_=w2_bf[:, PACK * P : PACK * (N + P)]
                )
            else:
                h_codes = keep.tile([P, hi - lo], U32, name=f"h_codes{lo}", align_bytes=64)
                h_plane = keep.tile([P, hi - lo], U8, name=f"h_plane{lo}", align_bytes=64)
                nc.vector.quantize_mx(out=h_codes[:].bitcast(FP8X4), scales=h_plane[:], in_=h_bf[group][:])
            last = g >= FIRST_SHARED_GROUP
            res = psum2.tile([P, N // P, hi - lo], F32, name="res")
            banks = (res, psum1.tile([P, N // P, hi - lo], F32, name="acc")) if last else (res, res)
            for u in range(N // P):
                nc.tensor.matmul_mx(
                    out=banks[u][:, u, :],
                    lhsT=w2_codes[:, u * P : (u + 1) * P].bitcast(FP8X4),
                    lhsT_scale=w2_plane[:, u * P : (u + 1) * P],
                    rhs=h_codes[:].bitcast(FP8X4),
                    rhs_scale=h_plane[:],
                    start=True,
                    stop=True,
                )
            products[g] = banks

        def store(g, on_vector=False):
            group = GROUPS[g]
            lo, hi = CHUNKS[group[0]][0], CHUNKS[group[-1]][1]
            banks = products[g]
            staged = keep.tile([P, N // P, hi - lo], F32, name=f"staged{lo}")
            if g >= FIRST_SHARED_GROUP:
                nc.scalar.copy(out=staged[:, 0, :], in_=banks[0][:, 0, :])
                nc.vector.tensor_copy(out=staged[:, 1, :], in_=banks[1][:, 1, :])
            elif on_vector:
                nc.vector.tensor_copy(out=staged[:], in_=banks[0][:])
            else:
                nc.scalar.copy(out=staged[:], in_=banks[0][:])
            nc.sync.dma_start(out=out_rows[:, :, lo:hi], in_=staged[:])

        cast_w2(0)
        cast_w2(1)
        quantize_w2(0)
        first_layer(0)
        first_layer(1)
        relu(0)
        first_layer(2)
        relu(1)
        second_layer(0)
        first_layer(3)
        relu(2)
        store(0)
        second_layer(1)
        first_layer(4)
        relu(3)
        store(1)
        first_layer(5)
        relu(4)
        second_layer(2)
        relu(5)
        first_layer(6)
        store(2)
        second_layer(3)
        first_layer(7)
        relu(6)
        second_layer(4)
        relu(7)
        store(3)
        second_layer(5)
        second_layer(6)
        store(4)
        store(5)
        store(6)
